import numpy as np
import ml_dtypes


def mxq(x, axis, fmt="e4m3"):
    dtype, down = {"e4m3": (ml_dtypes.float8_e4m3fn, 7), "e5m2": (ml_dtypes.float8_e5m2, 14)}[fmt]
    v = np.moveaxis(np.asarray(x, np.float32).astype(ml_dtypes.bfloat16).astype(np.float64), axis, -1)
    blocks = v.reshape(v.shape[:-1] + (-1, 32))
    amax = np.abs(blocks).max(-1, keepdims=True)
    byte = np.maximum(np.where(amax > 0, np.frexp(amax)[1] - 1 + 127, 0) - down, 1)
    scale = np.exp2(byte - 127.0)
    codes = (blocks / scale).astype(np.float32).astype(dtype).astype(np.float64)
    return np.moveaxis((codes * scale).reshape(v.shape), -1, axis)


WIDE = False


def mx_kscale(k):
    if not WIDE:
        return np.ones(k)
    levels = np.array([10, -10, 5, -5, 0])
    if k % 512:
        return np.exp2(np.random.permutation(np.resize(levels, k // 32))).repeat(32)
    a = np.empty((k // 512, 16))
    for p in range(k // 512):
        a[p, :8] = np.random.permutation(np.resize(levels, 8))
        for g in range(8):
            far = levels[np.abs(levels - a[p, g]) >= 10]
            a[p, g + 8] = far[np.random.randint(len(far))]
    return np.exp2(a.ravel()).repeat(32)


def f64(x):
    return np.asarray(x).astype(np.float64)


def striped(idx):
    return np.tile(idx.reshape(-1, 16).T, (8, 1)).astype(np.uint16)


def unstriped(offs):
    return offs[:16].T.reshape(-1).astype(np.int64)


def striped8(idx):
    return np.concatenate([x.reshape(-1, 16).T for x in idx]).astype(np.uint16)


def runs(offs, k):
    lists = np.stack([offs[16 * r : 16 * r + 16].T.reshape(-1) for r in range(8)]).astype(np.int64)
    return lists[np.arange(k) % 512 // 64]


def pack_weight(w):
    k, n = w.shape
    w = f64(np.asarray(w, np.float32).astype(ml_dtypes.bfloat16)).reshape(k // 32, 32, n)
    amax = np.abs(w).max(1)
    byte = np.clip(np.where(amax > 0, np.frexp(amax)[1] - 1 + 127 - 7, 1), 1, 254)
    scaled = (w * np.exp2(127.0 - byte)[:, None, :]).reshape(k, n).astype(np.float32)
    words = np.ascontiguousarray(scaled.reshape(k // 512, 128, 4, n).transpose(0, 1, 3, 2)).astype(ml_dtypes.float8_e4m3fn).view(np.uint8)
    return words, np.ascontiguousarray(byte.astype(np.uint8).reshape(k // 512, 16, n))


def unpack_weight(words, scales):
    g, p, n, _ = words.shape
    vals = np.ascontiguousarray(words).view(ml_dtypes.float8_e4m3fn).astype(np.float64) * np.repeat(np.exp2(scales.astype(np.float64) - 127.0), 8, axis=1)[..., None]
    return vals.transpose(0, 1, 3, 2).reshape(g * 512, n)


K, T, S, H, G, W = 512, 1024, 512, 512, 2048, 256


def setup_inputs():
    n = np.random.standard_normal
    s = mx_kscale(K)[:, None]
    packed_xT = pack_weight(n((K, T)) * s)
    packed_dT = pack_weight(n((K, G)) / s)
    perm = np.stack([np.random.permutation(S) for _ in range(8)])
    return {
        "x_words": packed_xT[0],
        "x_scales": packed_xT[1],
        "w1": (n((K, H)) / np.sqrt(K) / s).astype(np.float32),
        "gs": (np.random.uniform(0.5, 1.5, (K, 1)) * s).astype(np.float32),
        "d_words": packed_dT[0],
        "d_scales": packed_dT[1],
        "offs": striped(np.random.permutation(T)[:S]),
        "k1": striped8(np.random.randint(0, G, (8, H))),
        "k2": striped8(np.random.randint(0, G, (8, H))),
        "two": striped(np.random.permutation(T)[:S]),
        "n1": striped8(perm[:, :W]),
        "n2": striped8(perm[:, W:]),
        "n3": striped8(np.stack([np.random.permutation(S) for _ in range(8)])),
    }


def reference(x_words, x_scales, w1, gs, d_words, d_scales, offs, k1, k2, two, n1, n2, n3):
    d_k1 = unpack_weight(d_words, d_scales)[np.arange(K)[:, None], runs(k1, K)]
    xq = unpack_weight(x_words, x_scales)[:, unstriped(offs)]
    y = mxq(f64(w1), 0, "e4m3").T @ xq
    z = f64(gs) * y
    d_k2 = unpack_weight(d_words, d_scales)[np.arange(K)[:, None], runs(k2, K)]
    x_two = unpack_weight(x_words, x_scales)[:, unstriped(two)]
    h = 0.0625 * ((d_k1.T @ mxq(z, 0, "e4m3") + d_k2.T @ x_two))
    pa = h[np.arange(H)[:, None], runs(n1, H)]
    pb = h[np.arange(H)[:, None], runs(n2, H)]
    rb = pa - pb
    ra = pa + pb
    ds = np.zeros((H, S))
    ds[np.arange(H)[:, None], runs(n1, H)] = ra
    dt = ds.copy()
    dt[np.arange(H)[:, None], runs(n2, H)] = rb
    return np.maximum(dt, dt[np.arange(H)[:, None], runs(n3, H)])

@@ -1,0 +1,196 @@
+from contextlib import ExitStack
+
+import concourse.mybir as mybir
+
+K, T, S, H, G, W = 512, 1024, 512, 512, 2048, 256
+FLOPS = 3 * 2 * K * H * S
+
+F32 = mybir.dt.float32
+BF16 = mybir.dt.bfloat16
+I32 = mybir.dt.int32
+U32 = mybir.dt.uint32
+U16 = mybir.dt.uint16
+U8 = mybir.dt.uint8
+FP8X4 = mybir.dt.float8_e4m3fn_x4
+ADD = mybir.AluOpType.add
+MULT = mybir.AluOpType.mult
+MAX = mybir.AluOpType.max
+COPY = mybir.ActivationFunctionType.Copy
+
+P = 128
+PACK = 4
+QUAD = 32
+TILES = H // P
+
+
+def tile_picked_cmixihaarh_none_p_kernel(tc, x_words, x_scales, w1, gs, d_words, d_scales, offs, k1, k2, two, n1, n2, n3, out):
+    nc = tc.nc
+    with ExitStack() as ctx:
+        lists = ctx.enter_context(tc.tile_pool(name="lists", bufs=1))
+        keep = ctx.enter_context(tc.tile_pool(name="keep", bufs=1))
+        reuse = ctx.enter_context(tc.tile_pool(name="reuse", bufs=1))
+        psum = ctx.enter_context(tc.psum_pool(name="psum", bufs=1))
+
+        def load_list(src, name):
+            tile = lists.tile(list(src.shape), U16, name=name)
+            nc.sync.dma_start(tile[:], src)
+            return tile
+
+        def sb(shape, dtype, name):
+            return keep.tile(shape, dtype, name=name, align_bytes=64)
+
+        def load_scale_rows(table, src):
+            for q in range(4):
+                rows = src[0, 4 * q : 4 * q + 4, :].bitcast(I32)
+                nc.sync.dma_start(table[QUAD * q : QUAD * (q + 1), :].bitcast(I32), rows.unsqueeze(0).to_broadcast([8] + list(rows.shape)))
+
+        xs_tab = sb([P, T], U8, "xs_tab")
+        ds_tab = sb([P, G], U8, "ds_tab")
+        load_scale_rows(xs_tab, x_scales)
+        offs_t = load_list(offs, "offs_t")
+        xw_tab = sb([P, T], U32, "xw_tab")
+        nc.scalar.dma_start(xw_tab[:].bitcast(I32), x_words[0].rearrange("p n r -> p (n r)").bitcast(I32))
+        two_t = load_list(two, "two_t")
+        w_rows = w1.rearrange("(p j) c -> p j c", j=PACK)
+        w_raw = []
+        for u in range(2):
+            part = sb([P, PACK, H // 2], F32, f"w_raw{u}")
+            nc.scalar.dma_start(part[:], w_rows[:, :, u * (H // 2) : (u + 1) * (H // 2)])
+            w_raw.append(part)
+        k1_t = load_list(k1, "k1_t")
+        load_scale_rows(ds_tab, d_scales)
+        k2_t = load_list(k2, "k2_t")
+        dw_tab = sb([P, G], U32, "dw_tab")
+        nc.sync.dma_start(dw_tab[:].bitcast(I32), d_words[0].rearrange("p n r -> p (n r)").bitcast(I32))
+        gs_t = sb([P, PACK], F32, "gs_t")
+        nc.gpsimd.dma_start(gs_t[:], gs.rearrange("(p t) o -> p (t o)", t=PACK))
+        n1_t = load_list(n1, "n1_t")
+        n2_t = load_list(n2, "n2_t")
+        n3_t = load_list(n3, "n3_t")
+
+        def gather(dtype, table, offsets, name):
+            tile = sb([P, S], dtype, name)
+            nc.vector.tensor_copy(tile[:], table[:].indirect(offsets[:]))
+            return tile
+
+        xq_s = gather(U8, xs_tab, offs_t, "xq_s")
+        x2_s = gather(U8, xs_tab, two_t, "x2_s")
+        xq_w = gather(U32, xw_tab, offs_t, "xq_w")
+
+        w_bf = reuse.tile([P, H * PACK], BF16, name="w_bf", offset=0, align_bytes=64)
+        w_view = w_bf[:].rearrange("p (t m j) -> p m t j", t=PACK, j=PACK)
+        for u in range(2):
+            nc.scalar.copy(w_view[:, u * 64 : (u + 1) * 64], w_raw[u][:].rearrange("p j (m t) -> p m t j", t=PACK))
+
+        x2_w = gather(U32, xw_tab, two_t, "x2_w")
+
+        w_codes = sb([P, H], U32, "w_codes")
+        w_plane = sb([P, H], U8, "w_plane")
+        nc.vector.quantize_mx(w_codes[:].bitcast(FP8X4), w_plane[:], w_bf[:])
+
+        y_banks = []
+        for t in range(PACK):
+            bank = psum.tile([P, S], F32, name=f"y{t}")
+            cols = slice(t * P, (t + 1) * P)
+            nc.tensor.matmul_mx(bank[:], lhsT=w_codes[:, cols].bitcast(FP8X4), lhsT_scale=w_plane[:, cols],
+                                rhs=xq_w[:].bitcast(FP8X4), rhs_scale=xq_s[:], start=True, stop=True)
+            y_banks.append(bank)
+        z_rows = sb([P, PACK, S], BF16, "z_rows")
+        for t in range(PACK):
+            nc.scalar.activation(z_rows[:, t, :], y_banks[t][:], COPY, scale=gs_t[:, t : t + 1])
+        z_bf = sb([P, S * PACK], BF16, "z_bf")
+        nc.scalar.copy(z_bf[:].rearrange("p (c i t) -> p c t i", i=4, t=PACK), z_rows[:].rearrange("p t (c i) -> p c t i", i=4))
+
+        d_plane = sb([P, 2 * H], U8, "d_plane")
+        ds1_picked = gather(U8, ds_tab, k1_t, "ds1_picked")
+        ds2_picked = reuse.tile([P, H], U8, name="ds2_picked", offset=0, align_bytes=64)
+        d2_picked = reuse.tile([P, H], U32, name="d2_picked", offset=512, align_bytes=64)
+        d1_picked = reuse.tile([P, H], U32, name="d1_picked", offset=2560, align_bytes=64)
+        nc.vector.tensor_copy(ds2_picked[:], ds_tab[:].indirect(k2_t[:]))
+        nc.vector.tensor_copy(d2_picked[:], dw_tab[:].indirect(k2_t[:]))
+        for u, picked in enumerate((ds1_picked, ds2_picked)):
+            nc.vector.tensor_copy(
+                d_plane[:, u * H : (u + 1) * H].bitcast(I32).rearrange("p (t a b) -> p t a b", t=TILES, b=2),
+                picked[:].bitcast(I32).rearrange("p (a t b) -> p t a b", t=TILES, b=2))
+        for r in (2, 3):
+            nc.sync.dma_start(d_plane[r:P:QUAD, :].bitcast(I32), d_plane[16 + r : P : QUAD, :].bitcast(I32))
+        nc.vector.tensor_copy(d1_picked[:], dw_tab[:].indirect(k1_t[:]))
+
+        def deal(picked, name):
+            tile = sb([P, H], U32, name)
+            nc.vector.tensor_copy(tile[:].bitcast(I32).rearrange("p (t a b) -> p t a b", t=TILES, b=8),
+                                  picked[:].bitcast(I32).rearrange("p (a t b) -> p t a b", t=TILES, b=8))
+            return tile
+
+        d2_w = deal(d2_picked, "d2_w")
+        d1_w = deal(d1_picked, "d1_w")
+
+        z_codes = sb([P, S], U32, "z_codes")
+        z_plane = sb([P, S], U8, "z_plane")
+        nc.vector.quantize_mx(z_codes[:].bitcast(FP8X4), z_plane[:], z_bf[:])
+
+        spans = [(0, 0, W), (0, W, S)] + [(t, 0, S) for t in range(1, TILES)]
+        h_banks = []
+        for n, (t, c0, c1) in enumerate(spans):
+            bank = psum.tile([P, c1 - c0], F32, name=f"h{n}", tag="y0" if n == 0 else f"h{n}")
+            cols = slice(t * P, (t + 1) * P)
+            nc.tensor.matmul_mx(bank[:], lhsT=d2_w[:, cols].bitcast(FP8X4), lhsT_scale=d_plane[:, H + t * P : H + (t + 1) * P],
+                                rhs=x2_w[:, c0:c1].bitcast(FP8X4), rhs_scale=x2_s[:, c0:c1], start=True, stop=False)
+            h_banks.append(bank)
+        for n, (t, c0, c1) in enumerate(spans):
+            cols = slice(t * P, (t + 1) * P)
+            nc.tensor.matmul_mx(h_banks[n][:], lhsT=d1_w[:, cols].bitcast(FP8X4), lhsT_scale=d_plane[:, cols],
+                                rhs=z_codes[:, c0:c1].bitcast(FP8X4), rhs_scale=z_plane[:, c0:c1], start=False, stop=True)
+
+        out_rows = out.rearrange("(a t b) c -> t a b c", t=TILES, b=8)
+        dts, peers = [], []
+
+        def pair_up(t):
+            h = sb([P, S], F32, f"h_sb{t}")
+            pa = sb([P, W], F32, f"pa{t}")
+            pb = sb([P, W], F32, f"pb{t}")
+            neg_pb = sb([P, W], F32, f"neg_pb{t}")
+            if t == 0:
+                nc.scalar.activation(h[:, 0:W], h_banks[0][:], COPY, scale=0.0625)
+                nc.vector.tensor_scalar_mul(h[:, W:S], h_banks[1][:], 0.0625)
+                nc.scalar.activation(pa[:], h[:].indirect(n1_t[:]), COPY)
+                nc.vector.tensor_scalar(neg_pb[:], h[:].indirect(n2_t[:]), -1.0, 0.0, MULT, ADD)
+                nc.scalar.activation(pb[:], neg_pb[:], COPY, scale=-1.0)
+            else:
+                nc.scalar.activation(h[:], h_banks[t + 1][:], COPY, scale=0.0625)
+                nc.scalar.activation(pa[:], h[:].indirect(n1_t[:]), COPY)
+                nc.scalar.activation(pb[:], h[:].indirect(n2_t[:]), COPY)
+                nc.scalar.activation(neg_pb[:], pb[:], COPY, scale=-1.0)
+            return pa, pb, neg_pb
+
+        def finish(t):
+            res = sb([P, S], F32, f"res{t}")
+            nc.vector.tensor_tensor(res[:], dts[t][:], peers[t][:], MAX)
+            nc.sync.dma_start(out_rows[t], res[:])
+
+        pairs = pair_up(0)
+        for t in range(TILES):
+            pa, pb, neg_pb = pairs
+            dt = sb([P, S], F32, f"dt{t}")
+            dts.append(dt)
+            puts = [(n1_t, pb), (n2_t, neg_pb)]
+            if t == 0:
+                puts = [puts[1], puts[0]]
+            nc.vector.tensor_tensor(dt[:].indirect(puts[0][0][:]), pa[:], puts[0][1][:], ADD)
+            if t > 0:
+                finish(t - 1)
+            nc.vector.tensor_tensor(dt[:].indirect(puts[1][0][:]), pa[:], puts[1][1][:], ADD)
+            if t + 1 < TILES:
+                pairs = pair_up(t + 1)
+                peer = sb([P, S], F32, f"peer{t}")
+                for u in range(2):
+                    nc.scalar.activation(peer[:, u * W : (u + 1) * W], dt[:].indirect(n3_t[:, u * 16 : (u + 1) * 16]), COPY)
+                peers.append(peer)
+        last = TILES - 1
+        halves = [sb([P, W], F32, f"peer_half{u}") for u in range(2)]
+        nc.vector.tensor_copy(halves[0][:], dts[last][:].indirect(n3_t[:, 0:16]))
+        nc.scalar.activation(halves[1][:], dts[last][:].indirect(n3_t[:, 16:32]), COPY)
+        for u in range(2):
+            res = sb([P, W], F32, f"res_half{u}")
+            nc.vector.tensor_tensor(res[:], dts[last][:, u * W : (u + 1) * W], halves[u][:], MAX)
+            nc.sync.dma_start(out_rows[last][:, :, u * W : (u + 1) * W], res[:])

@@ -48,18 +48,18 @@ def tile_picked_cmixihaarh_none_p_kernel(tc, x_words, x_scales, w1, gs, d_words,
         ds_tab = sb([P, G], U8, "ds_tab")
         load_scale_rows(xs_tab, x_scales)
         offs_t = load_list(offs, "offs_t")
-        xw_tab = sb([P, T], U32, "xw_tab")
-        nc.scalar.dma_start(xw_tab[:].bitcast(I32), x_words[0].rearrange("p n r -> p (n r)").bitcast(I32))
         two_t = load_list(two, "two_t")
+        xw_tab = sb([P, T], U32, "xw_tab")
+        nc.sync.dma_start(xw_tab[:].bitcast(I32), x_words[0].rearrange("p n r -> p (n r)").bitcast(I32))
         w_rows = w1.rearrange("(p j) c -> p j c", j=PACK)
         w_raw = []
         for u in range(2):
             part = sb([P, PACK, H // 2], F32, f"w_raw{u}")
-            nc.scalar.dma_start(part[:], w_rows[:, :, u * (H // 2) : (u + 1) * (H // 2)])
+            nc.sync.dma_start(part[:], w_rows[:, :, u * (H // 2) : (u + 1) * (H // 2)])
             w_raw.append(part)
         k1_t = load_list(k1, "k1_t")
-        load_scale_rows(ds_tab, d_scales)
         k2_t = load_list(k2, "k2_t")
+        load_scale_rows(ds_tab, d_scales)
         dw_tab = sb([P, G], U32, "dw_tab")
         nc.sync.dma_start(dw_tab[:].bitcast(I32), d_words[0].rearrange("p n r -> p (n r)").bitcast(I32))
         gs_t = sb([P, PACK], F32, "gs_t")
@@ -95,11 +95,15 @@ def tile_picked_cmixihaarh_none_p_kernel(tc, x_words, x_scales, w1, gs, d_words,
             nc.tensor.matmul_mx(bank[:], lhsT=w_codes[:, cols].bitcast(FP8X4), lhsT_scale=w_plane[:, cols],
                                 rhs=xq_w[:].bitcast(FP8X4), rhs_scale=xq_s[:], start=True, stop=True)
             y_banks.append(bank)
-        z_rows = sb([P, PACK, S], BF16, "z_rows")
-        for t in range(PACK):
-            nc.scalar.activation(z_rows[:, t, :], y_banks[t][:], COPY, scale=gs_t[:, t : t + 1])
-        z_bf = sb([P, S * PACK], BF16, "z_bf")
-        nc.scalar.copy(z_bf[:].rearrange("p (c i t) -> p c t i", i=4, t=PACK), z_rows[:].rearrange("p t (c i) -> p c t i", i=4))
+        z_bf = []
+        for u in range(2):
+            cols = slice(u * W, (u + 1) * W)
+            z_rows = sb([P, PACK, W], BF16, f"z_rows{u}")
+            for t in range(PACK):
+                nc.scalar.activation(z_rows[:, t, :], y_banks[t][:, cols], COPY, scale=gs_t[:, t : t + 1])
+            woven = sb([P, W * PACK], BF16, f"z_bf{u}")
+            nc.scalar.copy(woven[:].rearrange("p (c i t) -> p c t i", i=4, t=PACK), z_rows[:].rearrange("p t (c i) -> p c t i", i=4))
+            z_bf.append(woven)
 
         d_plane = sb([P, 2 * H], U8, "d_plane")
         ds1_picked = gather(U8, ds_tab, k1_t, "ds1_picked")
@@ -127,70 +131,68 @@ def tile_picked_cmixihaarh_none_p_kernel(tc, x_words, x_scales, w1, gs, d_words,
 
         z_codes = sb([P, S], U32, "z_codes")
         z_plane = sb([P, S], U8, "z_plane")
-        nc.vector.quantize_mx(z_codes[:].bitcast(FP8X4), z_plane[:], z_bf[:])
+        for u in range(2):
+            cols = slice(u * W, (u + 1) * W)
+            nc.vector.quantize_mx(z_codes[:, cols].bitcast(FP8X4), z_plane[:, cols], z_bf[u][:])
 
-        spans = [(0, 0, W), (0, W, S)] + [(t, 0, S) for t in range(1, TILES)]
-        h_banks = []
-        for n, (t, c0, c1) in enumerate(spans):
-            bank = psum.tile([P, c1 - c0], F32, name=f"h{n}", tag="y0" if n == 0 else f"h{n}")
-            cols = slice(t * P, (t + 1) * P)
-            nc.tensor.matmul_mx(bank[:], lhsT=d2_w[:, cols].bitcast(FP8X4), lhsT_scale=d_plane[:, H + t * P : H + (t + 1) * P],
-                                rhs=x2_w[:, c0:c1].bitcast(FP8X4), rhs_scale=x2_s[:, c0:c1], start=True, stop=False)
+        def product(bank, t, c0, c1, which, start):
+            rows = slice(t * P, (t + 1) * P)
+            codes, plane0, mov, mov_plane = ((d1_w, 0, z_codes, z_plane), (d2_w, H, x2_w, x2_s))[which]
+            nc.tensor.matmul_mx(bank[:], lhsT=codes[:, rows].bitcast(FP8X4), lhsT_scale=d_plane[:, plane0 + t * P : plane0 + (t + 1) * P],
+                                rhs=mov[:, c0:c1].bitcast(FP8X4), rhs_scale=mov_plane[:, c0:c1], start=start, stop=not start)
+
+        h_banks = [psum.tile([P, W], F32, name="h0a", tag="y0"), psum.tile([P, W], F32, name="h0b")]
+        for u in range(2):
+            product(h_banks[u], 0, u * W, (u + 1) * W, 1, True)
+        for u in range(2):
+            product(h_banks[u], 0, u * W, (u + 1) * W, 0, False)
+        for t in range(1, TILES):
+            bank = psum.tile([P, S], F32, name=f"h{t}")
+            product(bank, t, 0, S, 0, True)
+            product(bank, t, 0, S, 1, False)
             h_banks.append(bank)
-        for n, (t, c0, c1) in enumerate(spans):
-            cols = slice(t * P, (t + 1) * P)
-            nc.tensor.matmul_mx(h_banks[n][:], lhsT=d1_w[:, cols].bitcast(FP8X4), lhsT_scale=d_plane[:, cols],
-                                rhs=z_codes[:, c0:c1].bitcast(FP8X4), rhs_scale=z_plane[:, c0:c1], start=False, stop=True)
 
         out_rows = out.rearrange("(a t b) c -> t a b c", t=TILES, b=8)
-        dts, peers = [], []
-
-        def pair_up(t):
-            h = sb([P, S], F32, f"h_sb{t}")
-            pa = sb([P, W], F32, f"pa{t}")
-            pb = sb([P, W], F32, f"pb{t}")
-            neg_pb = sb([P, W], F32, f"neg_pb{t}")
-            if t == 0:
-                nc.scalar.activation(h[:, 0:W], h_banks[0][:], COPY, scale=0.0625)
-                nc.vector.tensor_scalar_mul(h[:, W:S], h_banks[1][:], 0.0625)
-                nc.scalar.activation(pa[:], h[:].indirect(n1_t[:]), COPY)
-                nc.vector.tensor_scalar(neg_pb[:], h[:].indirect(n2_t[:]), -1.0, 0.0, MULT, ADD)
-                nc.scalar.activation(pb[:], neg_pb[:], COPY, scale=-1.0)
-            else:
-                nc.scalar.activation(h[:], h_banks[t + 1][:], COPY, scale=0.0625)
-                nc.scalar.activation(pa[:], h[:].indirect(n1_t[:]), COPY)
-                nc.scalar.activation(pb[:], h[:].indirect(n2_t[:]), COPY)
-                nc.scalar.activation(neg_pb[:], pb[:], COPY, scale=-1.0)
-            return pa, pb, neg_pb
-
-        def finish(t):
-            res = sb([P, S], F32, f"res{t}")
-            nc.vector.tensor_tensor(res[:], dts[t][:], peers[t][:], MAX)
-            nc.sync.dma_start(out_rows[t], res[:])
-
-        pairs = pair_up(0)
+        pas, pbs, negs, dts = [], [], [], []
         for t in range(TILES):
-            pa, pb, neg_pb = pairs
-            dt = sb([P, S], F32, f"dt{t}")
-            dts.append(dt)
-            puts = [(n1_t, pb), (n2_t, neg_pb)]
-            if t == 0:
-                puts = [puts[1], puts[0]]
-            nc.vector.tensor_tensor(dt[:].indirect(puts[0][0][:]), pa[:], puts[0][1][:], ADD)
-            if t > 0:
-                finish(t - 1)
-            nc.vector.tensor_tensor(dt[:].indirect(puts[1][0][:]), pa[:], puts[1][1][:], ADD)
-            if t + 1 < TILES:
-                pairs = pair_up(t + 1)
-                peer = sb([P, S], F32, f"peer{t}")
-                for u in range(2):
-                    nc.scalar.activation(peer[:, u * W : (u + 1) * W], dt[:].indirect(n3_t[:, u * 16 : (u + 1) * 16]), COPY)
-                peers.append(peer)
-        last = TILES - 1
-        halves = [sb([P, W], F32, f"peer_half{u}") for u in range(2)]
-        nc.vector.tensor_copy(halves[0][:], dts[last][:].indirect(n3_t[:, 0:16]))
-        nc.scalar.activation(halves[1][:], dts[last][:].indirect(n3_t[:, 16:32]), COPY)
-        for u in range(2):
-            res = sb([P, W], F32, f"res_half{u}")
-            nc.vector.tensor_tensor(res[:], dts[last][:, u * W : (u + 1) * W], halves[u][:], MAX)
-            nc.sync.dma_start(out_rows[last][:, :, u * W : (u + 1) * W], res[:])
+            pas.append(sb([P, W], F32, f"pa{t}"))
+            pbs.append(sb([P, W], F32, f"pb{t}"))
+            negs.append(sb([P, W], F32, f"neg_pb{t}"))
+            dts.append(sb([P, S], F32, f"dt{t}"))
+
+        def put_sum(t):
+            nc.vector.tensor_tensor(dts[t][:].indirect(n1_t[:]), pas[t][:], pbs[t][:], ADD)
+
+        def put_difference(t):
+            nc.vector.tensor_tensor(dts[t][:].indirect(n2_t[:]), pas[t][:], negs[t][:], ADD)
+
+        def negate(t):
+            nc.scalar.activation(negs[t][:], pbs[t][:], COPY, scale=-1.0)
+            put_difference(t)
+
+        h = keep.tile([P, S], F32, name="h_first", tag="h_sb1", align_bytes=64)
+        nc.scalar.activation(h[:, 0:W], h_banks[0][:], COPY, scale=0.0625)
+        nc.vector.tensor_scalar_mul(h[:, W:S], h_banks[1][:], 0.0625)
+        nc.scalar.activation(pas[0][:], h[:].indirect(n1_t[:]), COPY)
+        nc.vector.tensor_scalar(negs[0][:], h[:].indirect(n2_t[:]), -1.0, 0.0, MULT, ADD)
+        put_difference(0)
+        nc.scalar.activation(pbs[0][:], negs[0][:], COPY, scale=-1.0)
+        put_sum(0)
+        for t in range(1, TILES):
+            h = sb([P, S], F32, f"h_sb{t}")
+            nc.scalar.activation(h[:], h_banks[t + 1][:], COPY, scale=0.0625)
+            nc.scalar.activation(pas[t][:], h[:].indirect(n1_t[:]), COPY)
+            nc.scalar.activation(pbs[t][:], h[:].indirect(n2_t[:]), COPY)
+            put_sum(t)
+            if t > 1:
+                negate(t - 1)
+        negate(TILES - 1)
+        for t in range(TILES):
+            peer = sb([P, S], F32, f"peer{t}")
+            for u in range(2):
+                nc.scalar.activation(peer[:, u * W : (u + 1) * W], dts[t][:].indirect(n3_t[:, u * 16 : (u + 1) * 16]), COPY)
+            step = W if t == TILES - 1 else S
+            for c0 in range(0, S, step):
+                res = sb([P, step], F32, f"res{t}_{c0}")
+                nc.vector.tensor_tensor(res[:], dts[t][:, c0 : c0 + step], peer[:, c0 : c0 + step], MAX)
+                nc.sync.dma_start(out_rows[t][:, :, c0 : c0 + step], res[:])

@@ -21,6 +21,8 @@ P = 128
 PACK = 4
 QUAD = 32
 TILES = H // P
+Z_PIECES = ((0, 256), (256, 384), (384, 512))
+W_PIECES = ((0, 256), (256, 384), (384, 512))
 
 
 def tile_picked_cmixihaarh_none_p_kernel(tc, x_words, x_scales, w1, gs, d_words, d_scales, offs, k1, k2, two, n1, n2, n3, out):
@@ -29,6 +31,8 @@ def tile_picked_cmixihaarh_none_p_kernel(tc, x_words, x_scales, w1, gs, d_words,
         lists = ctx.enter_context(tc.tile_pool(name="lists", bufs=1))
         keep = ctx.enter_context(tc.tile_pool(name="keep", bufs=1))
         reuse = ctx.enter_context(tc.tile_pool(name="reuse", bufs=1))
+        late = ctx.enter_context(tc.tile_pool(name="late", bufs=1))
+        after_d = ctx.enter_context(tc.tile_pool(name="after_d", bufs=1))
         psum = ctx.enter_context(tc.psum_pool(name="psum", bufs=1))
 
         def load_list(src, name):
@@ -39,28 +43,30 @@ def tile_picked_cmixihaarh_none_p_kernel(tc, x_words, x_scales, w1, gs, d_words,
         def sb(shape, dtype, name):
             return keep.tile(shape, dtype, name=name, align_bytes=64)
 
-        def load_scale_rows(table, src):
-            for q in range(4):
-                rows = src[0, 4 * q : 4 * q + 4, :].bitcast(I32)
-                nc.sync.dma_start(table[QUAD * q : QUAD * (q + 1), :].bitcast(I32), rows.unsqueeze(0).to_broadcast([8] + list(rows.shape)))
+        def load_scale_rows(table, src, places):
+            for r, place in enumerate(places):
+                nc.sync.dma_start(table[place:P:QUAD, :].bitcast(I32), src[0, r:16:4, :].bitcast(I32))
 
         xs_tab = sb([P, T], U8, "xs_tab")
         ds_tab = sb([P, G], U8, "ds_tab")
-        load_scale_rows(xs_tab, x_scales)
+        nc.gpsimd.memset(xs_tab[:].bitcast(I32), 0)
+        nc.vector.memset(ds_tab[:].bitcast(I32), 0)
         offs_t = load_list(offs, "offs_t")
         two_t = load_list(two, "two_t")
+        load_scale_rows(xs_tab, x_scales, (0, 1, 2, 3))
         xw_tab = sb([P, T], U32, "xw_tab")
-        nc.sync.dma_start(xw_tab[:].bitcast(I32), x_words[0].rearrange("p n r -> p (n r)").bitcast(I32))
         w_rows = w1.rearrange("(p j) c -> p j c", j=PACK)
         w_raw = []
-        for u in range(2):
-            part = sb([P, PACK, H // 2], F32, f"w_raw{u}")
-            nc.sync.dma_start(part[:], w_rows[:, :, u * (H // 2) : (u + 1) * (H // 2)])
+        for c0, c1 in W_PIECES:
+            part = sb([P, PACK, c1 - c0], F32, f"w_raw{c0}")
+            nc.sync.dma_start(part[:], w_rows[:, :, c0:c1])
             w_raw.append(part)
+            if c0 == 0:
+                nc.sync.dma_start(xw_tab[:].bitcast(I32), x_words[0].rearrange("p n r -> p (n r)").bitcast(I32))
         k1_t = load_list(k1, "k1_t")
         k2_t = load_list(k2, "k2_t")
-        load_scale_rows(ds_tab, d_scales)
-        dw_tab = sb([P, G], U32, "dw_tab")
+        load_scale_rows(ds_tab, d_scales, (0, 1, 18, 19))
+        dw_tab = after_d.tile([P, G], U32, name="dw_tab", offset=0, align_bytes=64)
         nc.sync.dma_start(dw_tab[:].bitcast(I32), d_words[0].rearrange("p n r -> p (n r)").bitcast(I32))
         gs_t = sb([P, PACK], F32, "gs_t")
         nc.gpsimd.dma_start(gs_t[:], gs.rearrange("(p t) o -> p (t o)", t=PACK))
@@ -79,14 +85,15 @@ def tile_picked_cmixihaarh_none_p_kernel(tc, x_words, x_scales, w1, gs, d_words,
 
         w_bf = reuse.tile([P, H * PACK], BF16, name="w_bf", offset=0, align_bytes=64)
         w_view = w_bf[:].rearrange("p (t m j) -> p m t j", t=PACK, j=PACK)
-        for u in range(2):
-            nc.scalar.copy(w_view[:, u * 64 : (u + 1) * 64], w_raw[u][:].rearrange("p j (m t) -> p m t j", t=PACK))
+        for (c0, c1), part in zip(W_PIECES, w_raw):
+            nc.scalar.copy(w_view[:, c0 // PACK : c1 // PACK], part[:].rearrange("p j (m t) -> p m t j", t=PACK))
 
         x2_w = gather(U32, xw_tab, two_t, "x2_w")
 
         w_codes = sb([P, H], U32, "w_codes")
         w_plane = sb([P, H], U8, "w_plane")
-        nc.vector.quantize_mx(w_codes[:].bitcast(FP8X4), w_plane[:], w_bf[:])
+        for c0, c1 in ((0, P), (P, H)):
+            nc.vector.quantize_mx(w_codes[:, c0:c1].bitcast(FP8X4), w_plane[:, c0:c1], w_bf[:, PACK * c0 : PACK * c1])
 
         y_banks = []
         for t in range(PACK):
@@ -95,57 +102,56 @@ def tile_picked_cmixihaarh_none_p_kernel(tc, x_words, x_scales, w1, gs, d_words,
             nc.tensor.matmul_mx(bank[:], lhsT=w_codes[:, cols].bitcast(FP8X4), lhsT_scale=w_plane[:, cols],
                                 rhs=xq_w[:].bitcast(FP8X4), rhs_scale=xq_s[:], start=True, stop=True)
             y_banks.append(bank)
+        z_rows = sb([P, PACK, S], BF16, "z_rows")
+        for t in range(PACK):
+            nc.scalar.activation(z_rows[:, t, :], y_banks[t][:], COPY, scale=gs_t[:, t : t + 1])
         z_bf = []
-        for u in range(2):
-            cols = slice(u * W, (u + 1) * W)
-            z_rows = sb([P, PACK, W], BF16, f"z_rows{u}")
-            for t in range(PACK):
-                nc.scalar.activation(z_rows[:, t, :], y_banks[t][:, cols], COPY, scale=gs_t[:, t : t + 1])
-            woven = sb([P, W * PACK], BF16, f"z_bf{u}")
-            nc.scalar.copy(woven[:].rearrange("p (c i t) -> p c t i", i=4, t=PACK), z_rows[:].rearrange("p t (c i) -> p c t i", i=4))
+        for c0, c1 in Z_PIECES:
+            woven = late.tile([P, (c1 - c0) * PACK], BF16, name=f"z_bf{c0}", offset=c0 * 8, align_bytes=64)
+            nc.scalar.copy(woven[:].rearrange("p (c i t) -> p c t i", i=4, t=PACK),
+                           z_rows[:, :, c0:c1].rearrange("p t (c i) -> p c t i", i=4))
             z_bf.append(woven)
 
         d_plane = sb([P, 2 * H], U8, "d_plane")
         ds1_picked = gather(U8, ds_tab, k1_t, "ds1_picked")
         ds2_picked = reuse.tile([P, H], U8, name="ds2_picked", offset=0, align_bytes=64)
-        d2_picked = reuse.tile([P, H], U32, name="d2_picked", offset=512, align_bytes=64)
-        d1_picked = reuse.tile([P, H], U32, name="d1_picked", offset=2560, align_bytes=64)
+        dw_picked = reuse.tile([P, 2 * H], U32, name="dw_picked", offset=512, align_bytes=64)
         nc.vector.tensor_copy(ds2_picked[:], ds_tab[:].indirect(k2_t[:]))
-        nc.vector.tensor_copy(d2_picked[:], dw_tab[:].indirect(k2_t[:]))
+        nc.vector.tensor_copy(dw_picked[:, H : 2 * H], dw_tab[:].indirect(k2_t[:]))
         for u, picked in enumerate((ds1_picked, ds2_picked)):
             nc.vector.tensor_copy(
                 d_plane[:, u * H : (u + 1) * H].bitcast(I32).rearrange("p (t a b) -> p t a b", t=TILES, b=2),
                 picked[:].bitcast(I32).rearrange("p (a t b) -> p t a b", t=TILES, b=2))
         for r in (2, 3):
             nc.sync.dma_start(d_plane[r:P:QUAD, :].bitcast(I32), d_plane[16 + r : P : QUAD, :].bitcast(I32))
-        nc.vector.tensor_copy(d1_picked[:], dw_tab[:].indirect(k1_t[:]))
+        nc.vector.tensor_copy(dw_picked[:, 0:H], dw_tab[:].indirect(k1_t[:]))
 
-        def deal(picked, name):
-            tile = sb([P, H], U32, name)
-            nc.vector.tensor_copy(tile[:].bitcast(I32).rearrange("p (t a b) -> p t a b", t=TILES, b=8),
-                                  picked[:].bitcast(I32).rearrange("p (a t b) -> p t a b", t=TILES, b=8))
-            return tile
+        by_tile = dw_picked[:].bitcast(I32).rearrange("p (l a t b) -> p l t a b", l=2, t=TILES, b=8)
+        d_first = sb([P, 2 * P], U32, "d_first")
+        for l in (1, 0):
+            nc.vector.tensor_copy(d_first[:, l * P : (l + 1) * P].bitcast(I32).rearrange("p (a b) -> p a b", b=8), by_tile[:, l, 0])
 
-        d2_w = deal(d2_picked, "d2_w")
-        d1_w = deal(d1_picked, "d1_w")
-
-        z_codes = sb([P, S], U32, "z_codes")
+        z_codes = after_d.tile([P, S], U32, name="z_codes", offset=0, align_bytes=64)
         z_plane = sb([P, S], U8, "z_plane")
-        for u in range(2):
-            cols = slice(u * W, (u + 1) * W)
-            nc.vector.quantize_mx(z_codes[:, cols].bitcast(FP8X4), z_plane[:, cols], z_bf[u][:])
+        for (c0, c1), woven in zip(Z_PIECES, z_bf):
+            nc.vector.quantize_mx(z_codes[:, c0:c1].bitcast(FP8X4), z_plane[:, c0:c1], woven[:])
+
+        d_rest = late.tile([P, 2, H - P], U32, name="d_rest", offset=1024, align_bytes=64)
+        nc.vector.tensor_copy(d_rest[:].bitcast(I32).rearrange("p l (t a b) -> p l t a b", a=16, b=8), by_tile[:, :, 1:TILES])
 
         def product(bank, t, c0, c1, which, start):
-            rows = slice(t * P, (t + 1) * P)
-            codes, plane0, mov, mov_plane = ((d1_w, 0, z_codes, z_plane), (d2_w, H, x2_w, x2_s))[which]
-            nc.tensor.matmul_mx(bank[:], lhsT=codes[:, rows].bitcast(FP8X4), lhsT_scale=d_plane[:, plane0 + t * P : plane0 + (t + 1) * P],
+            codes = d_first[:, which * P : (which + 1) * P] if t == 0 else d_rest[:, which, (t - 1) * P : t * P]
+            plane0 = which * H
+            mov, mov_plane = ((z_codes, z_plane), (x2_w, x2_s))[which]
+            nc.tensor.matmul_mx(bank[:], lhsT=codes.bitcast(FP8X4), lhsT_scale=d_plane[:, plane0 + t * P : plane0 + (t + 1) * P],
                                 rhs=mov[:, c0:c1].bitcast(FP8X4), rhs_scale=mov_plane[:, c0:c1], start=start, stop=not start)
 
-        h_banks = [psum.tile([P, W], F32, name="h0a", tag="y0"), psum.tile([P, W], F32, name="h0b")]
-        for u in range(2):
-            product(h_banks[u], 0, u * W, (u + 1) * W, 1, True)
-        for u in range(2):
-            product(h_banks[u], 0, u * W, (u + 1) * W, 0, False)
+        first_banks = [psum.tile([P, c1 - c0], F32, name=f"h0_{c0}", tag=f"y{n}") for n, (c0, c1) in enumerate(Z_PIECES)]
+        for (c0, c1), bank in zip(Z_PIECES, first_banks):
+            opener = 1 if c0 == 0 else 0
+            product(bank, 0, c0, c1, opener, True)
+            product(bank, 0, c0, c1, 1 - opener, False)
+        h_banks = [None]
         for t in range(1, TILES):
             bank = psum.tile([P, S], F32, name=f"h{t}")
             product(bank, t, 0, S, 0, True)
@@ -171,8 +177,8 @@ def tile_picked_cmixihaarh_none_p_kernel(tc, x_words, x_scales, w1, gs, d_words,
             put_difference(t)
 
         h = keep.tile([P, S], F32, name="h_first", tag="h_sb1", align_bytes=64)
-        nc.scalar.activation(h[:, 0:W], h_banks[0][:], COPY, scale=0.0625)
-        nc.vector.tensor_scalar_mul(h[:, W:S], h_banks[1][:], 0.0625)
+        for (c0, c1), bank in zip(Z_PIECES, first_banks):
+            nc.scalar.activation(h[:, c0:c1], bank[:], COPY, scale=0.0625)
         nc.scalar.activation(pas[0][:], h[:].indirect(n1_t[:]), COPY)
         nc.vector.tensor_scalar(negs[0][:], h[:].indirect(n2_t[:]), -1.0, 0.0, MULT, ADD)
         put_difference(0)
@@ -180,7 +186,7 @@ def tile_picked_cmixihaarh_none_p_kernel(tc, x_words, x_scales, w1, gs, d_words,
         put_sum(0)
         for t in range(1, TILES):
             h = sb([P, S], F32, f"h_sb{t}")
-            nc.scalar.activation(h[:], h_banks[t + 1][:], COPY, scale=0.0625)
+            nc.scalar.activation(h[:], h_banks[t][:], COPY, scale=0.0625)
             nc.scalar.activation(pas[t][:], h[:].indirect(n1_t[:]), COPY)
             nc.scalar.activation(pbs[t][:], h[:].indirect(n2_t[:]), COPY)
             put_sum(t)

@@ -22,7 +22,7 @@ PACK = 4
 QUAD = 32
 TILES = H // P
 Z_PIECES = ((0, 256), (256, 384), (384, 512))
-W_PIECES = ((0, 256), (256, 384), (384, 512))
+W_PIECES = ((0, 128), (128, 384), (384, 512))
 
 
 def tile_picked_cmixihaarh_none_p_kernel(tc, x_words, x_scales, w1, gs, d_words, d_scales, offs, k1, k2, two, n1, n2, n3, out):
@@ -52,8 +52,6 @@ def tile_picked_cmixihaarh_none_p_kernel(tc, x_words, x_scales, w1, gs, d_words,
         nc.gpsimd.memset(xs_tab[:].bitcast(I32), 0)
         nc.vector.memset(ds_tab[:].bitcast(I32), 0)
         offs_t = load_list(offs, "offs_t")
-        two_t = load_list(two, "two_t")
-        load_scale_rows(xs_tab, x_scales, (0, 1, 2, 3))
         xw_tab = sb([P, T], U32, "xw_tab")
         w_rows = w1.rearrange("(p j) c -> p j c", j=PACK)
         w_raw = []
@@ -62,6 +60,8 @@ def tile_picked_cmixihaarh_none_p_kernel(tc, x_words, x_scales, w1, gs, d_words,
             nc.sync.dma_start(part[:], w_rows[:, :, c0:c1])
             w_raw.append(part)
             if c0 == 0:
+                two_t = load_list(two, "two_t")
+                load_scale_rows(xs_tab, x_scales, (0, 1, 2, 3))
                 nc.sync.dma_start(xw_tab[:].bitcast(I32), x_words[0].rearrange("p n r -> p (n r)").bitcast(I32))
         k1_t = load_list(k1, "k1_t")
         k2_t = load_list(k2, "k2_t")
@@ -184,9 +184,16 @@ def tile_picked_cmixihaarh_none_p_kernel(tc, x_words, x_scales, w1, gs, d_words,
         put_difference(0)
         nc.scalar.activation(pbs[0][:], negs[0][:], COPY, scale=-1.0)
         put_sum(0)
+        def empty(t):
+            rows = sb([P, S], F32, f"h_sb{t}")
+            nc.scalar.activation(rows[:], h_banks[t][:], COPY, scale=0.0625)
+            return rows
+
+        ahead = empty(1)
         for t in range(1, TILES):
-            h = sb([P, S], F32, f"h_sb{t}")
-            nc.scalar.activation(h[:], h_banks[t][:], COPY, scale=0.0625)
+            h = ahead
+            if t + 1 < TILES:
+                ahead = empty(t + 1)
             nc.scalar.activation(pas[t][:], h[:].indirect(n1_t[:]), COPY)
             nc.scalar.activation(pbs[t][:], h[:].indirect(n2_t[:]), COPY)
             put_sum(t)

from contextlib import ExitStack

import concourse.mybir as mybir

K, T, S, H, G, W = 512, 1024, 512, 512, 2048, 256
FLOPS = 3 * 2 * K * H * S

F32 = mybir.dt.float32
BF16 = mybir.dt.bfloat16
I32 = mybir.dt.int32
U32 = mybir.dt.uint32
U16 = mybir.dt.uint16
U8 = mybir.dt.uint8
FP8X4 = mybir.dt.float8_e4m3fn_x4
ADD = mybir.AluOpType.add
MULT = mybir.AluOpType.mult
MAX = mybir.AluOpType.max
COPY = mybir.ActivationFunctionType.Copy

P = 128
PACK = 4
QUAD = 32
TILES = H // P
Z_PIECES = ((0, 256), (256, 384), (384, 512))
W_PIECES = ((0, 128), (128, 384), (384, 512))


def tile_picked_cmixihaarh_none_p_kernel(tc, x_words, x_scales, w1, gs, d_words, d_scales, offs, k1, k2, two, n1, n2, n3, out):
    nc = tc.nc
    with ExitStack() as ctx:
        lists = ctx.enter_context(tc.tile_pool(name="lists", bufs=1))
        keep = ctx.enter_context(tc.tile_pool(name="keep", bufs=1))
        reuse = ctx.enter_context(tc.tile_pool(name="reuse", bufs=1))
        late = ctx.enter_context(tc.tile_pool(name="late", bufs=1))
        after_d = ctx.enter_context(tc.tile_pool(name="after_d", bufs=1))
        psum = ctx.enter_context(tc.psum_pool(name="psum", bufs=1))

        def load_list(src, name):
            tile = lists.tile(list(src.shape), U16, name=name)
            nc.sync.dma_start(tile[:], src)
            return tile

        def sb(shape, dtype, name):
            return keep.tile(shape, dtype, name=name, align_bytes=64)

        def load_scale_rows(table, src, places):
            for r, place in enumerate(places):
                nc.sync.dma_start(table[place:P:QUAD, :].bitcast(I32), src[0, r:16:4, :].bitcast(I32))

        xs_tab = sb([P, T], U8, "xs_tab")
        ds_tab = sb([P, G], U8, "ds_tab")
        nc.gpsimd.memset(xs_tab[:].bitcast(I32), 0)
        nc.vector.memset(ds_tab[:].bitcast(I32), 0)
        offs_t = load_list(offs, "offs_t")
        xw_tab = sb([P, T], U32, "xw_tab")
        w_rows = w1.rearrange("(p j) c -> p j c", j=PACK)
        w_raw = []
        for c0, c1 in W_PIECES:
            part = sb([P, PACK, c1 - c0], F32, f"w_raw{c0}")
            nc.sync.dma_start(part[:], w_rows[:, :, c0:c1])
            w_raw.append(part)
            if c0 == 0:
                two_t = load_list(two, "two_t")
                load_scale_rows(xs_tab, x_scales, (0, 1, 2, 3))
                nc.sync.dma_start(xw_tab[:].bitcast(I32), x_words[0].rearrange("p n r -> p (n r)").bitcast(I32))
        k1_t = load_list(k1, "k1_t")
        k2_t = load_list(k2, "k2_t")
        load_scale_rows(ds_tab, d_scales, (0, 1, 18, 19))
        dw_tab = after_d.tile([P, G], U32, name="dw_tab", offset=0, align_bytes=64)
        nc.sync.dma_start(dw_tab[:].bitcast(I32), d_words[0].rearrange("p n r -> p (n r)").bitcast(I32))
        gs_t = sb([P, PACK], F32, "gs_t")
        nc.gpsimd.dma_start(gs_t[:], gs.rearrange("(p t) o -> p (t o)", t=PACK))
        n1_t = load_list(n1, "n1_t")
        n2_t = load_list(n2, "n2_t")
        n3_t = load_list(n3, "n3_t")

        def gather(dtype, table, offsets, name):
            tile = sb([P, S], dtype, name)
            nc.vector.tensor_copy(tile[:], table[:].indirect(offsets[:]))
            return tile

        xq_s = gather(U8, xs_tab, offs_t, "xq_s")
        x2_s = gather(U8, xs_tab, two_t, "x2_s")
        xq_w = gather(U32, xw_tab, offs_t, "xq_w")

        w_bf = reuse.tile([P, H * PACK], BF16, name="w_bf", offset=0, align_bytes=64)
        w_view = w_bf[:].rearrange("p (t m j) -> p m t j", t=PACK, j=PACK)
        for (c0, c1), part in zip(W_PIECES, w_raw):
            nc.scalar.copy(w_view[:, c0 // PACK : c1 // PACK], part[:].rearrange("p j (m t) -> p m t j", t=PACK))

        x2_w = gather(U32, xw_tab, two_t, "x2_w")

        w_codes = sb([P, H], U32, "w_codes")
        w_plane = sb([P, H], U8, "w_plane")
        for c0, c1 in ((0, P), (P, H)):
            nc.vector.quantize_mx(w_codes[:, c0:c1].bitcast(FP8X4), w_plane[:, c0:c1], w_bf[:, PACK * c0 : PACK * c1])

        y_banks = []
        for t in range(PACK):
            bank = psum.tile([P, S], F32, name=f"y{t}")
            cols = slice(t * P, (t + 1) * P)
            nc.tensor.matmul_mx(bank[:], lhsT=w_codes[:, cols].bitcast(FP8X4), lhsT_scale=w_plane[:, cols],
                                rhs=xq_w[:].bitcast(FP8X4), rhs_scale=xq_s[:], start=True, stop=True)
            y_banks.append(bank)
        z_rows = sb([P, PACK, S], BF16, "z_rows")
        for t in range(PACK):
            nc.scalar.activation(z_rows[:, t, :], y_banks[t][:], COPY, scale=gs_t[:, t : t + 1])
        z_bf = []
        for c0, c1 in Z_PIECES:
            woven = late.tile([P, (c1 - c0) * PACK], BF16, name=f"z_bf{c0}", offset=c0 * 8, align_bytes=64)
            nc.scalar.copy(woven[:].rearrange("p (c i t) -> p c t i", i=4, t=PACK),
                           z_rows[:, :, c0:c1].rearrange("p t (c i) -> p c t i", i=4))
            z_bf.append(woven)

        d_plane = sb([P, 2 * H], U8, "d_plane")
        ds1_picked = gather(U8, ds_tab, k1_t, "ds1_picked")
        ds2_picked = reuse.tile([P, H], U8, name="ds2_picked", offset=0, align_bytes=64)
        dw_picked = reuse.tile([P, 2 * H], U32, name="dw_picked", offset=512, align_bytes=64)
        nc.vector.tensor_copy(ds2_picked[:], ds_tab[:].indirect(k2_t[:]))
        nc.vector.tensor_copy(dw_picked[:, H : 2 * H], dw_tab[:].indirect(k2_t[:]))
        for u, picked in enumerate((ds1_picked, ds2_picked)):
            nc.vector.tensor_copy(
                d_plane[:, u * H : (u + 1) * H].bitcast(I32).rearrange("p (t a b) -> p t a b", t=TILES, b=2),
                picked[:].bitcast(I32).rearrange("p (a t b) -> p t a b", t=TILES, b=2))
        for r in (2, 3):
            nc.sync.dma_start(d_plane[r:P:QUAD, :].bitcast(I32), d_plane[16 + r : P : QUAD, :].bitcast(I32))
        nc.vector.tensor_copy(dw_picked[:, 0:H], dw_tab[:].indirect(k1_t[:]))

        by_tile = dw_picked[:].bitcast(I32).rearrange("p (l a t b) -> p l t a b", l=2, t=TILES, b=8)
        d_first = sb([P, 2 * P], U32, "d_first")
        for l in (1, 0):
            nc.vector.tensor_copy(d_first[:, l * P : (l + 1) * P].bitcast(I32).rearrange("p (a b) -> p a b", b=8), by_tile[:, l, 0])

        z_codes = after_d.tile([P, S], U32, name="z_codes", offset=0, align_bytes=64)
        z_plane = sb([P, S], U8, "z_plane")
        for (c0, c1), woven in zip(Z_PIECES, z_bf):
            nc.vector.quantize_mx(z_codes[:, c0:c1].bitcast(FP8X4), z_plane[:, c0:c1], woven[:])

        d_rest = late.tile([P, 2, H - P], U32, name="d_rest", offset=1024, align_bytes=64)
        nc.vector.tensor_copy(d_rest[:].bitcast(I32).rearrange("p l (t a b) -> p l t a b", a=16, b=8), by_tile[:, :, 1:TILES])

        def product(bank, t, c0, c1, which, start):
            codes = d_first[:, which * P : (which + 1) * P] if t == 0 else d_rest[:, which, (t - 1) * P : t * P]
            plane0 = which * H
            mov, mov_plane = ((z_codes, z_plane), (x2_w, x2_s))[which]
            nc.tensor.matmul_mx(bank[:], lhsT=codes.bitcast(FP8X4), lhsT_scale=d_plane[:, plane0 + t * P : plane0 + (t + 1) * P],
                                rhs=mov[:, c0:c1].bitcast(FP8X4), rhs_scale=mov_plane[:, c0:c1], start=start, stop=not start)

        first_banks = [psum.tile([P, c1 - c0], F32, name=f"h0_{c0}", tag=f"y{n}") for n, (c0, c1) in enumerate(Z_PIECES)]
        for (c0, c1), bank in zip(Z_PIECES, first_banks):
            opener = 1 if c0 == 0 else 0
            product(bank, 0, c0, c1, opener, True)
            product(bank, 0, c0, c1, 1 - opener, False)
        h_banks = [None]
        for t in range(1, TILES):
            bank = psum.tile([P, S], F32, name=f"h{t}")
            product(bank, t, 0, S, 0, True)
            product(bank, t, 0, S, 1, False)
            h_banks.append(bank)

        out_rows = out.rearrange("(a t b) c -> t a b c", t=TILES, b=8)
        pas, pbs, negs, dts = [], [], [], []
        for t in range(TILES):
            pas.append(sb([P, W], F32, f"pa{t}"))
            pbs.append(sb([P, W], F32, f"pb{t}"))
            negs.append(sb([P, W], F32, f"neg_pb{t}"))
            dts.append(sb([P, S], F32, f"dt{t}"))

        def put_sum(t):
            nc.vector.tensor_tensor(dts[t][:].indirect(n1_t[:]), pas[t][:], pbs[t][:], ADD)

        def put_difference(t):
            nc.vector.tensor_tensor(dts[t][:].indirect(n2_t[:]), pas[t][:], negs[t][:], ADD)

        def negate(t):
            nc.scalar.activation(negs[t][:], pbs[t][:], COPY, scale=-1.0)
            put_difference(t)

        h = keep.tile([P, S], F32, name="h_first", tag="h_sb1", align_bytes=64)
        for (c0, c1), bank in zip(Z_PIECES, first_banks):
            nc.scalar.activation(h[:, c0:c1], bank[:], COPY, scale=0.0625)
        nc.scalar.activation(pas[0][:], h[:].indirect(n1_t[:]), COPY)
        nc.vector.tensor_scalar(negs[0][:], h[:].indirect(n2_t[:]), -1.0, 0.0, MULT, ADD)
        put_difference(0)
        nc.scalar.activation(pbs[0][:], negs[0][:], COPY, scale=-1.0)
        put_sum(0)
        def empty(t):
            rows = sb([P, S], F32, f"h_sb{t}")
            nc.scalar.activation(rows[:], h_banks[t][:], COPY, scale=0.0625)
            return rows

        ahead = empty(1)
        for t in range(1, TILES):
            h = ahead
            if t + 1 < TILES:
                ahead = empty(t + 1)
            nc.scalar.activation(pas[t][:], h[:].indirect(n1_t[:]), COPY)
            nc.scalar.activation(pbs[t][:], h[:].indirect(n2_t[:]), COPY)
            put_sum(t)
            if t > 1:
                negate(t - 1)
        negate(TILES - 1)
        for t in range(TILES):
            peer = sb([P, S], F32, f"peer{t}")
            for u in range(2):
                nc.scalar.activation(peer[:, u * W : (u + 1) * W], dts[t][:].indirect(n3_t[:, u * 16 : (u + 1) * 16]), COPY)
            step = W if t == TILES - 1 else S
            for c0 in range(0, S, step):
                res = sb([P, step], F32, f"res{t}_{c0}")
                nc.vector.tensor_tensor(res[:], dts[t][:, c0 : c0 + step], peer[:, c0 : c0 + step], MAX)
                nc.sync.dma_start(out_rows[t][:, :, c0 : c0 + step], res[:])
